import numpy as np
import ml_dtypes


def mxq(x, axis, fmt="e4m3"):
    dtype, down = {"e4m3": (ml_dtypes.float8_e4m3fn, 7), "e5m2": (ml_dtypes.float8_e5m2, 14)}[fmt]
    v = np.moveaxis(np.asarray(x, np.float32).astype(ml_dtypes.bfloat16).astype(np.float64), axis, -1)
    blocks = v.reshape(v.shape[:-1] + (-1, 32))
    amax = np.abs(blocks).max(-1, keepdims=True)
    byte = np.maximum(np.where(amax > 0, np.frexp(amax)[1] - 1 + 127, 0) - down, 1)
    scale = np.exp2(byte - 127.0)
    codes = (blocks / scale).astype(np.float32).astype(dtype).astype(np.float64)
    return np.moveaxis((codes * scale).reshape(v.shape), -1, axis)


WIDE = False


def mx_kscale(k):
    if not WIDE:
        return np.ones(k)
    levels = np.array([10, -10, 5, -5, 0])
    if k % 512:
        return np.exp2(np.random.permutation(np.resize(levels, k // 32))).repeat(32)
    a = np.empty((k // 512, 16))
    for p in range(k // 512):
        a[p, :8] = np.random.permutation(np.resize(levels, 8))
        for g in range(8):
            far = levels[np.abs(levels - a[p, g]) >= 10]
            a[p, g + 8] = far[np.random.randint(len(far))]
    return np.exp2(a.ravel()).repeat(32)


def f64(x):
    return np.asarray(x).astype(np.float64)


def striped(idx):
    return np.tile(np.asarray(idx).reshape(-1, 16).T, (8, 1)).astype(np.uint16)


def unstriped(offs):
    return offs[:16].T.reshape(-1).astype(np.int64)


def striped8(idx):
    return np.asarray(idx).reshape(8, -1, 16).transpose(0, 2, 1).reshape(128, -1).astype(np.uint16)


def unstriped8(offs):
    return offs.reshape(8, 16, -1).transpose(0, 2, 1).reshape(8, -1).astype(np.int64)


def pick8(x, idx, run):
    r = np.arange(len(x))
    return x[r[:, None], idx[r % (8 * run) // run]]


E2M1 = np.array([0.0, 0.5, 1.0, 1.5, 2.0, 3.0, 4.0, 6.0, -0.0, -0.5, -1.0, -1.5, -2.0, -3.0, -4.0, -6.0])


def pack_weight(w, fmt):
    k, n = w.shape
    w = f64(np.asarray(w, np.float32).astype(ml_dtypes.bfloat16)).reshape(k // 32, 32, n)
    amax = np.abs(w).max(1)
    if fmt == "e4m3":
        byte = np.frexp(amax)[1] - 1 + 127 - 7
    else:
        mant, ex = np.frexp(amax / 6.0)
        byte = np.where(mant > 0.5, ex, ex - 1) + 127
    byte = np.clip(np.where(amax > 0, byte, 1), 1, 254)
    scaled = (w * np.exp2(127.0 - byte)[:, None, :]).reshape(k, n).astype(np.float32)
    by_word = np.ascontiguousarray(scaled.reshape(k // 512, 128, 4, n).transpose(0, 1, 3, 2))
    if fmt == "e4m3":
        words = by_word.astype(ml_dtypes.float8_e4m3fn).view(np.uint8)
    else:
        c = by_word.astype(ml_dtypes.float4_e2m1fn).view(np.uint8) & 0xF
        words = (c[..., 0::2] | (c[..., 1::2] << 4)).reshape(k // 512, 128, 2 * n)
    return np.ascontiguousarray(words), np.ascontiguousarray(byte.astype(np.uint8).reshape(k // 512, 16, n))


def unpack_weight(words, scales, fmt):
    g, _, n = scales.shape
    words = np.ascontiguousarray(words).reshape(g, 128, n, -1)
    if fmt == "e4m3":
        vals = words.view(ml_dtypes.float8_e4m3fn).astype(np.float64)
    else:
        nib = np.empty((g, 128, n, 4), np.uint8)
        nib[..., 0::2] = words & 0xF
        nib[..., 1::2] = words >> 4
        vals = E2M1[nib]
    vals = vals * np.repeat(np.exp2(scales.astype(np.float64) - 127.0), 8, axis=1)[..., None]
    return vals.transpose(0, 1, 3, 2).reshape(g * 512, n)


K, J, R, T, F, G, I, O, N, S, Z = 512, 512, 512, 2048, 2048, 1024, 256, 256, 256, 512, 1024


def setup_inputs():
    n = np.random.standard_normal
    idx = np.random.permutation(T)[:J]
    idx2 = np.stack([np.random.permutation(F)[:R] for _ in range(8)])
    idx3 = np.stack([np.random.permutation(G)[:I] for _ in range(8)])
    idx4 = np.stack([np.random.permutation(R)[:I] for _ in range(8)])
    idx5 = np.stack([np.random.permutation(J)[:O] for _ in range(8)])
    idx6 = np.random.permutation(Z)[:O]
    fk = mx_kscale(K)
    fr = mx_kscale(R)
    fs = mx_kscale(S)
    xtp = pack_weight(n((K, T)) * fk[:, None], "e2m1")
    wbp = pack_weight(n((R, N)) * 1 / np.sqrt(R) / fr[:, None], "e4m3")
    xrp = pack_weight(n((S, Z)) / fs[:, None], "e4m3")
    wsp = pack_weight(n((S, N)) * 1 / np.sqrt(S) * fs[:, None], "e2m1")
    return {
        "xt_words": xtp[0],
        "xt_scales": xtp[1],
        "ua": (np.random.randint(-7, 8, (K, F)).astype(np.float64)).astype(np.float32),
        "ub": (np.random.randint(-7, 8, (K, G)).astype(np.float64)).astype(np.float32),
        "ha": ((np.random.randint(10, 25, (K, 1)) / 1024.0) / fk[:, None]).astype(np.float32),
        "hb": ((np.random.randint(4, 13, (K, 1)) / 1024.0) / fk[:, None]).astype(np.float32),
        "sa": (np.random.uniform(0.5, 1.6, (R, 1)) * fr[:, None]).astype(np.float32),
        "wb_words": wbp[0],
        "wb_scales": wbp[1],
        "xr_words": xrp[0],
        "xr_scales": xrp[1],
        "ws_words": wsp[0],
        "ws_scales": wsp[1],
        "offs": striped(idx),
        "offs2": striped8(idx2),
        "offs3": striped8(idx3),
        "offs4": striped8(idx4),
        "offs5": striped8(idx5),
        "offs6": striped(idx6),
    }


def reference(xt_words, xt_scales, ua, ub, ha, hb, sa, wb_words, wb_scales, xr_words, xr_scales, ws_words, ws_scales, offs, offs2, offs3, offs4, offs5, offs6):
    idx = unstriped(offs)
    idx2 = unstriped8(offs2)
    idx3 = unstriped8(offs3)
    idx4 = unstriped8(offs4)
    idx5 = unstriped8(offs5)
    idx6 = unstriped(offs6)
    xtu = unpack_weight(xt_words, xt_scales, "e2m1")
    wbu = unpack_weight(wb_words, wb_scales, "e4m3")
    xru = unpack_weight(xr_words, xr_scales, "e4m3")
    wsu = unpack_weight(ws_words, ws_scales, "e2m1")
    wcd = pick8(f64(ub), idx3, 64) * f64(hb)
    wcp = np.zeros((K, R))
    wcp[np.arange(K)[:, None], idx4[np.arange(K) % 512 // 64]] = wcd
    wc = pick8(f64(ua), idx2, 64) * f64(ha) + wcp
    wcq = mxq(wc, 0, "e4m3")
    xtidxg = xtu[:, idx]
    a = wcq.T @ xtidxg
    g1 = np.maximum(a, 0.0)
    hid = pick8(g1, idx5, 64) * f64(sa)
    hidq = mxq(hid, 0, "e4m3")
    xridx6g = xru[:, idx6]
    y = wbu.T @ hidq + wsu.T @ xridx6g
    return y

@@ -1,0 +1,216 @@
+from contextlib import ExitStack
+
+import concourse.mybir as mybir
+
+K, J, R, T, F, G, I, O, N, S, Z = 512, 512, 512, 2048, 2048, 1024, 256, 256, 256, 512, 1024
+FLOPS = 2 * K * R * J + 2 * R * N * O + 2 * S * N * O
+
+F32 = mybir.dt.float32
+BF16 = mybir.dt.bfloat16
+I32 = mybir.dt.int32
+U32 = mybir.dt.uint32
+U16 = mybir.dt.uint16
+U8 = mybir.dt.uint8
+FP8X4 = mybir.dt.float8_e4m3fn_x4
+FP4X4 = mybir.dt.float4_e2m1fn_x4
+ACT = mybir.ActivationFunctionType
+ALU = mybir.AluOpType
+
+P = 128
+PACK = 4
+HALF = O // 2
+
+
+def tile_picked_tokens_refinedsome_one_kept_reminder_plain_kernel(
+    tc, xt_words, xt_scales, ua, ub, ha, hb, sa, wb_words, wb_scales, xr_words, xr_scales,
+    ws_words, ws_scales, offs, offs2, offs3, offs4, offs5, offs6, out,
+):
+    nc = tc.nc
+    with ExitStack() as ctx:
+        keep = ctx.enter_context(tc.tile_pool(name="keep", bufs=1))
+        psum = ctx.enter_context(tc.psum_pool(name="psum", bufs=1))
+
+        def tiles(name, count, shape, dtype):
+            return [keep.tile(shape, dtype, name="%s%d" % (name, c), align_bytes=64) for c in range(count)]
+
+        def load_list(name, src):
+            lst = keep.tile(list(src.shape), U16, name=name)
+            nc.sync.dma_start(lst[:], src)
+            return lst
+
+        def load_column(queue, name, src):
+            col = keep.tile([P, PACK], F32, name=name)
+            queue.dma_start(col[:], src.rearrange("(p t) o -> p (t o)", t=PACK))
+            return col
+
+        def cleared_plane(name, width):
+            plane = keep.tile([P, width], U8, name=name, align_bytes=64)
+            nc.vector.memset(plane[:].bitcast(I32), 0)
+            return plane
+
+        def stage_plane(name, src, width, starts):
+            per = 4 // len(starts)
+            stage = keep.tile([P, per, width], U8, name=name, align_bytes=64)
+
+            def load(n):
+                rows = src[0, 4 * per * n : 4 * per * (n + 1), :].bitcast(I32).rearrange("(q i) c -> i q c", i=4)
+                nc.sync.dma_start(stage[starts[n] : starts[n] + 4].bitcast(I32), rows)
+
+            def spread(plane):
+                for q in range(4):
+                    p0 = starts[q // per]
+                    nc.vector.tensor_copy(
+                        plane[32 * q : 32 * q + 4, :].bitcast(I32), stage[p0 : p0 + 4, q % per, :].bitcast(I32)
+                    )
+
+            return load, spread
+
+        ua_rows = ua.rearrange("(p t) f -> t p f", t=PACK)
+        ub_rows = ub.rearrange("(p t) g -> t p g", t=PACK)
+        ua_sb = tiles("ua_sb", PACK, [P, F], F32)
+        ub_sb = tiles("ub_sb", PACK, [P, G], F32)
+        wcd = tiles("wcd", PACK, [P, I], F32)
+        wcp = tiles("wcp", PACK, [P, R], F32)
+        wca = tiles("wca", PACK, [P, R], F32)
+
+        nc.sync.dma_start(ub_sb[0][:], ub_rows[0])
+        hb_sb = load_column(nc.scalar, "hb_sb", hb)
+        ha_sb = load_column(nc.scalar, "ha_sb", ha)
+        l3 = load_list("l3", offs3)
+        l4 = load_list("l4", offs4)
+        l2 = load_list("l2", offs2)
+        nc.sync.dma_start(ua_sb[0][:], ua_rows[0])
+        nc.sync.dma_start(ub_sb[1][:], ub_rows[1])
+        xt_w = keep.tile([P, T], U16, name="xt_w", align_bytes=64)
+        nc.sync.dma_start(xt_w[:].bitcast(I32), xt_words[0].bitcast(I32))
+        l1 = load_list("l1", offs)
+        load_xt, spread_xt = stage_plane("xt_st", xt_scales, T, (0, 64))
+        load_xt(0)
+        load_xt(1)
+        nc.sync.dma_start(ua_sb[1][:], ua_rows[1])
+        load_wb, spread_wb = stage_plane("wb_st", wb_scales, N, (0,))
+        load_wb(0)
+        load_ws, spread_ws = stage_plane("ws_st", ws_scales, N, (0,))
+        load_ws(0)
+        nc.sync.dma_start(ub_sb[2][:], ub_rows[2])
+        l6 = load_list("l6", offs6)
+        load_xr, spread_xr = stage_plane("xr_st", xr_scales, Z, (0, 64))
+        load_xr(0)
+        load_xr(1)
+        nc.sync.dma_start(ua_sb[2][:], ua_rows[2])
+        nc.sync.dma_start(ub_sb[3][:], ub_rows[3])
+        nc.sync.dma_start(ua_sb[3][:], ua_rows[3])
+        xr_w = keep.tile([P, Z], U32, name="xr_w", align_bytes=64)
+        nc.sync.dma_start(xr_w[:].bitcast(I32), xr_words[0].rearrange("p z t -> p (z t)").bitcast(I32))
+        l5 = load_list("l5", offs5)
+        sa_sb = load_column(nc.sync, "sa_sb", sa)
+        ws_w = keep.tile([P, 2 * N], U8, name="ws_w", align_bytes=64)
+        nc.sync.dma_start(ws_w[:].bitcast(I32), ws_words[0].bitcast(I32))
+        wb_w = keep.tile([P, N], U32, name="wb_w", align_bytes=64)
+        nc.sync.dma_start(wb_w[:].bitcast(I32), wb_words[0].rearrange("p n t -> p (n t)").bitcast(I32))
+
+        for t in range(PACK):
+            nc.vector.memset(wcp[t][:], 0.0)
+        xt_s = cleared_plane("xt_s", T)
+        xr_s = cleared_plane("xr_s", Z)
+        wb_s = cleared_plane("wb_s", N)
+        ws_s = cleared_plane("ws_s", N)
+
+        wc_first = keep.tile([P, PACK - 1, R], BF16, name="wc_first", align_bytes=64)
+        wc_bf = tiles("wc_bf", PACK, [P, P, PACK], BF16)
+        wc_w = tiles("wc_w", PACK, [P, P], U32)
+        wc_s = tiles("wc_s", PACK, [P, P], U8)
+        acc = [psum.tile([P, J], F32, name="acc%d" % c) for c in range(PACK)]
+
+        def look_up_rows(t):
+            nc.scalar.activation(wcd[t][:], ub_sb[t][:].indirect(l3[:]), ACT.Copy, scale=hb_sb[:, t : t + 1])
+            nc.scalar.activation(wcp[t][:].indirect(l4[:]), wcd[t][:], ACT.Copy)
+            nc.scalar.activation(wca[t][:], ua_sb[t][:].indirect(l2[:]), ACT.Copy, scale=ha_sb[:, t : t + 1])
+            if t < PACK - 1:
+                nc.vector.tensor_tensor(wc_first[:, t, :], wca[t][:], wcp[t][:], ALU.add)
+
+        look_up_rows(0)
+        xg_w = keep.tile([P, J], U16, name="xg_w", align_bytes=64)
+        nc.vector.tensor_copy(xg_w[:], xt_w[:].indirect(l1[:]))
+        spread_xt(xt_s)
+        xg_s = keep.tile([P, J], U8, name="xg_s", align_bytes=64)
+        nc.vector.tensor_copy(xg_s[:], xt_s[:].indirect(l1[:]))
+        look_up_rows(1)
+        spread_wb(wb_s)
+        spread_ws(ws_s)
+        spread_xr(xr_s)
+        rg_s = keep.tile([P, O], U8, name="rg_s", align_bytes=64)
+        nc.vector.tensor_copy(rg_s[:], xr_s[:].indirect(l6[:]))
+        look_up_rows(2)
+        for c in range(PACK):
+            nc.vector.tensor_copy(
+                wc_bf[c][:, :, 0 : PACK - 1],
+                wc_first[:].rearrange("p t (m c) -> p c m t", c=PACK)[:, c, :, :],
+            )
+        last = PACK - 1
+        look_up_rows(last)
+        for c in range(PACK):
+            nc.vector.tensor_tensor(
+                wc_bf[c][:, :, last],
+                wca[last][:].rearrange("p (m c) -> p c m", c=PACK)[:, c, :],
+                wcp[last][:].rearrange("p (m c) -> p c m", c=PACK)[:, c, :],
+                ALU.add,
+            )
+            nc.vector.quantize_mx(
+                out=wc_w[c][:].bitcast(FP8X4), scales=wc_s[c][:],
+                in_=wc_bf[c][:].rearrange("p m t -> p (m t)"),
+            )
+            nc.tensor.matmul_mx(
+                out=acc[c][:], lhsT=wc_w[c][:].bitcast(FP8X4), lhsT_scale=wc_s[c][:],
+                rhs=xg_w[:].bitcast(FP4X4), rhs_scale=xg_s[:], start=True, stop=True,
+            )
+
+        g1 = tiles("g1", PACK, [P, J], F32)
+        hid = keep.tile([P, PACK, O], BF16, name="hid", align_bytes=64)
+        for c in range(PACK):
+            if c < 2:
+                nc.scalar.activation(g1[c][:], acc[c][:], ACT.Relu)
+            else:
+                nc.vector.tensor_scalar_max(g1[c][:], acc[c][:], 0.0)
+            pieces = [(0, O)] if c < PACK - 1 else [(0, HALF), (HALF, O)]
+            for lo, hi in pieces:
+                nc.scalar.activation(
+                    hid[:, c, lo:hi], g1[c][:].indirect(l5[:, lo // 16 : hi // 16]), ACT.Copy,
+                    scale=sa_sb[:, c : c + 1],
+                )
+
+        rg_w = keep.tile([P, O], U32, name="rg_w", tag="wc_bf3", align_bytes=64)
+        nc.vector.tensor_copy(rg_w[:], xr_w[:].indirect(l6[:]))
+        res = [[psum.tile([P, HALF], F32, name="res%d%d" % (u, h), tag="acc%d" % (2 * u + h)) for h in range(2)] for u in range(2)]
+        for u in range(2):
+            cols = slice(u * HALF, (u + 1) * HALF)
+            for h in range(2):
+                nc.tensor.matmul_mx(
+                    out=res[u][h][:], lhsT=ws_w[:, 2 * P * h : 2 * P * (h + 1)].bitcast(FP4X4),
+                    lhsT_scale=ws_s[:, P * h : P * (h + 1)],
+                    rhs=rg_w[:, cols].bitcast(FP8X4), rhs_scale=rg_s[:, cols], start=True, stop=False,
+                )
+
+        hid_bf = tiles("hid_bf", 2, [P, HALF, PACK], BF16)
+        hid_w = tiles("hid_w", 2, [P, HALF], U32)
+        hid_s = tiles("hid_s", 2, [P, HALF], U8)
+        out_sb = tiles("out_sb", 2, [P, 2, HALF], F32)
+        out_rows = out.rearrange("(h p) o -> p h o", p=P)
+        for u in range(2):
+            cols = slice(u * HALF, (u + 1) * HALF)
+            nc.vector.tensor_copy(hid_bf[u][:], hid[:, :, cols].rearrange("p c o -> p o c"))
+            nc.vector.quantize_mx(
+                out=hid_w[u][:].bitcast(FP8X4), scales=hid_s[u][:],
+                in_=hid_bf[u][:].rearrange("p o c -> p (o c)"),
+            )
+            for h in range(2):
+                nc.tensor.matmul_mx(
+                    out=res[u][h][:], lhsT=wb_w[:, P * h : P * (h + 1)].bitcast(FP8X4),
+                    lhsT_scale=wb_s[:, P * h : P * (h + 1)],
+                    rhs=hid_w[u][:].bitcast(FP8X4), rhs_scale=hid_s[u][:], start=False, stop=True,
+                )
+                if u == 1 and h == 1:
+                    nc.vector.tensor_copy(out_sb[u][:, h, :], res[u][h][:])
+                else:
+                    nc.scalar.copy(out_sb[u][:, h, :], res[u][h][:])
+            nc.sync.dma_start(out_rows[:, :, cols], out_sb[u][:])

@@ -78,21 +78,21 @@ def tile_picked_tokens_refinedsome_one_kept_reminder_plain_kernel(
         ha_sb = load_column(nc.scalar, "ha_sb", ha)
         l3 = load_list("l3", offs3)
         l4 = load_list("l4", offs4)
-        l2 = load_list("l2", offs2)
-        nc.sync.dma_start(ua_sb[0][:], ua_rows[0])
-        nc.sync.dma_start(ub_sb[1][:], ub_rows[1])
+        for t in range(1, PACK - 1):
+            nc.sync.dma_start(ub_sb[t][:], ub_rows[t])
         xt_w = keep.tile([P, T], U16, name="xt_w", align_bytes=64)
         nc.sync.dma_start(xt_w[:].bitcast(I32), xt_words[0].bitcast(I32))
         l1 = load_list("l1", offs)
         load_xt, spread_xt = stage_plane("xt_st", xt_scales, T, (0, 64))
         load_xt(0)
         load_xt(1)
-        nc.sync.dma_start(ua_sb[1][:], ua_rows[1])
+        nc.sync.dma_start(ua_sb[0][:], ua_rows[0])
+        l2 = load_list("l2", offs2)
         load_wb, spread_wb = stage_plane("wb_st", wb_scales, N, (0,))
         load_wb(0)
         load_ws, spread_ws = stage_plane("ws_st", ws_scales, N, (0,))
         load_ws(0)
-        nc.sync.dma_start(ub_sb[2][:], ub_rows[2])
+        nc.sync.dma_start(ua_sb[1][:], ua_rows[1])
         l6 = load_list("l6", offs6)
         load_xr, spread_xr = stage_plane("xr_st", xr_scales, Z, (0, 64))
         load_xr(0)
@@ -120,58 +120,72 @@ def tile_picked_tokens_refinedsome_one_kept_reminder_plain_kernel(
         wc_bf = tiles("wc_bf", PACK, [P, P, PACK], BF16)
         wc_w = tiles("wc_w", PACK, [P, P], U32)
         wc_s = tiles("wc_s", PACK, [P, P], U8)
-        acc = [psum.tile([P, J], F32, name="acc%d" % c) for c in range(PACK)]
+        acc = [[psum.tile([P, J // 2], F32, name="acc%d%d" % (c, v)) for v in range(2)] for c in range(PACK)]
 
-        def look_up_rows(t):
+        def place_details(t):
             nc.scalar.activation(wcd[t][:], ub_sb[t][:].indirect(l3[:]), ACT.Copy, scale=hb_sb[:, t : t + 1])
             nc.scalar.activation(wcp[t][:].indirect(l4[:]), wcd[t][:], ACT.Copy)
+
+        for t in range(PACK - 1):
+            place_details(t)
+
+        def look_up_rows(t):
             nc.scalar.activation(wca[t][:], ua_sb[t][:].indirect(l2[:]), ACT.Copy, scale=ha_sb[:, t : t + 1])
             if t < PACK - 1:
                 nc.vector.tensor_tensor(wc_first[:, t, :], wca[t][:], wcp[t][:], ALU.add)
 
-        look_up_rows(0)
         xg_w = keep.tile([P, J], U16, name="xg_w", align_bytes=64)
         nc.vector.tensor_copy(xg_w[:], xt_w[:].indirect(l1[:]))
         spread_xt(xt_s)
         xg_s = keep.tile([P, J], U8, name="xg_s", align_bytes=64)
         nc.vector.tensor_copy(xg_s[:], xt_s[:].indirect(l1[:]))
-        look_up_rows(1)
         spread_wb(wb_s)
         spread_ws(ws_s)
         spread_xr(xr_s)
         rg_s = keep.tile([P, O], U8, name="rg_s", align_bytes=64)
         nc.vector.tensor_copy(rg_s[:], xr_s[:].indirect(l6[:]))
-        look_up_rows(2)
+        for t in range(PACK - 1):
+            look_up_rows(t)
         for c in range(PACK):
             nc.vector.tensor_copy(
                 wc_bf[c][:, :, 0 : PACK - 1],
                 wc_first[:].rearrange("p t (m c) -> p c m t", c=PACK)[:, c, :, :],
             )
         last = PACK - 1
+        place_details(last)
         look_up_rows(last)
+        codes = wca[last][:].rearrange("p (m c) -> p m c", c=PACK)
+        details = wcp[last][:].rearrange("p (m c) -> p m c", c=PACK)
+        nc.vector.tensor_tensor(wc_bf[0][:, :, last], codes[:, :, 0], details[:, :, 0], ALU.add)
+        wc_last = keep.tile([P, PACK - 1, P], BF16, name="wc_last", align_bytes=64)
+        nc.vector.tensor_tensor(
+            wc_last[:].rearrange("p c m -> p m c"), codes[:, :, 1:PACK], details[:, :, 1:PACK], ALU.add
+        )
         for c in range(PACK):
-            nc.vector.tensor_tensor(
-                wc_bf[c][:, :, last],
-                wca[last][:].rearrange("p (m c) -> p c m", c=PACK)[:, c, :],
-                wcp[last][:].rearrange("p (m c) -> p c m", c=PACK)[:, c, :],
-                ALU.add,
-            )
+            if c == 2:
+                nc.vector.tensor_copy(wc_bf[c][:, :, last], wc_last[:, c - 1, :])
+            elif c > 0:
+                nc.scalar.copy(wc_bf[c][:, :, last], wc_last[:, c - 1, :])
             nc.vector.quantize_mx(
                 out=wc_w[c][:].bitcast(FP8X4), scales=wc_s[c][:],
                 in_=wc_bf[c][:].rearrange("p m t -> p (m t)"),
             )
-            nc.tensor.matmul_mx(
-                out=acc[c][:], lhsT=wc_w[c][:].bitcast(FP8X4), lhsT_scale=wc_s[c][:],
-                rhs=xg_w[:].bitcast(FP4X4), rhs_scale=xg_s[:], start=True, stop=True,
-            )
+            for v in range(2):
+                slots = slice(v * J // 2, (v + 1) * J // 2)
+                nc.tensor.matmul_mx(
+                    out=acc[c][v][:], lhsT=wc_w[c][:].bitcast(FP8X4), lhsT_scale=wc_s[c][:],
+                    rhs=xg_w[:, slots].bitcast(FP4X4), rhs_scale=xg_s[:, slots], start=True, stop=True,
+                )
 
         g1 = tiles("g1", PACK, [P, J], F32)
         hid = keep.tile([P, PACK, O], BF16, name="hid", align_bytes=64)
         for c in range(PACK):
-            if c < 2:
-                nc.scalar.activation(g1[c][:], acc[c][:], ACT.Relu)
-            else:
-                nc.vector.tensor_scalar_max(g1[c][:], acc[c][:], 0.0)
+            for v in range(2):
+                slots = slice(v * J // 2, (v + 1) * J // 2)
+                if c == 0:
+                    nc.scalar.activation(g1[c][:, slots], acc[c][v][:], ACT.Relu)
+                else:
+                    nc.vector.tensor_scalar_max(g1[c][:, slots], acc[c][v][:], 0.0)
             pieces = [(0, O)] if c < PACK - 1 else [(0, HALF), (HALF, O)]
             for lo, hi in pieces:
                 nc.scalar.activation(
@@ -179,9 +193,9 @@ def tile_picked_tokens_refinedsome_one_kept_reminder_plain_kernel(
                     scale=sa_sb[:, c : c + 1],
                 )
 
-        rg_w = keep.tile([P, O], U32, name="rg_w", tag="wc_bf3", align_bytes=64)
+        rg_w = keep.tile([P, O], U32, name="rg_w", tag="g10", align_bytes=64)
         nc.vector.tensor_copy(rg_w[:], xr_w[:].indirect(l6[:]))
-        res = [[psum.tile([P, HALF], F32, name="res%d%d" % (u, h), tag="acc%d" % (2 * u + h)) for h in range(2)] for u in range(2)]
+        res = [[psum.tile([P, HALF], F32, name="res%d%d" % (u, h), tag="acc%d%d" % (u, h)) for h in range(2)] for u in range(2)]
         for u in range(2):
             cols = slice(u * HALF, (u + 1) * HALF)
             for h in range(2):
@@ -194,8 +208,7 @@ def tile_picked_tokens_refinedsome_one_kept_reminder_plain_kernel(
         hid_bf = tiles("hid_bf", 2, [P, HALF, PACK], BF16)
         hid_w = tiles("hid_w", 2, [P, HALF], U32)
         hid_s = tiles("hid_s", 2, [P, HALF], U8)
-        out_sb = tiles("out_sb", 2, [P, 2, HALF], F32)
-        out_rows = out.rearrange("(h p) o -> p h o", p=P)
+        out_sb = [tiles("out_sb%d" % u, 2, [P, HALF], F32) for u in range(2)]
         for u in range(2):
             cols = slice(u * HALF, (u + 1) * HALF)
             nc.vector.tensor_copy(hid_bf[u][:], hid[:, :, cols].rearrange("p c o -> p o c"))
@@ -210,7 +223,8 @@ def tile_picked_tokens_refinedsome_one_kept_reminder_plain_kernel(
                     rhs=hid_w[u][:].bitcast(FP8X4), rhs_scale=hid_s[u][:], start=False, stop=True,
                 )
                 if u == 1 and h == 1:
-                    nc.vector.tensor_copy(out_sb[u][:, h, :], res[u][h][:])
+                    nc.vector.tensor_copy(out_sb[u][h][:], res[u][h][:])
                 else:
-                    nc.scalar.copy(out_sb[u][:, h, :], res[u][h][:])
-            nc.sync.dma_start(out_rows[:, :, cols], out_sb[u][:])
+                    nc.scalar.copy(out_sb[u][h][:], res[u][h][:])
+                queue = nc.scalar if (u == 1 and h == 0) else nc.sync
+                queue.dma_start(out[P * h : P * (h + 1), cols], out_sb[u][h][:])

@@ -76,6 +76,9 @@ def tile_picked_tokens_refinedsome_one_kept_reminder_plain_kernel(
         nc.sync.dma_start(ub_sb[0][:], ub_rows[0])
         hb_sb = load_column(nc.scalar, "hb_sb", hb)
         ha_sb = load_column(nc.scalar, "ha_sb", ha)
+        warm = keep.tile([P, 2], F32, name="warm")
+        nc.vector.memset(warm[:, 0:1], 0.0)
+        nc.scalar.activation(warm[:, 1:2], warm[:, 0:1], ACT.Copy)
         l3 = load_list("l3", offs3)
         l4 = load_list("l4", offs4)
         for t in range(1, PACK - 1):

from contextlib import ExitStack

import concourse.mybir as mybir

K, J, R, T, F, G, I, O, N, S, Z = 512, 512, 512, 2048, 2048, 1024, 256, 256, 256, 512, 1024
FLOPS = 2 * K * R * J + 2 * R * N * O + 2 * S * N * O

F32 = mybir.dt.float32
BF16 = mybir.dt.bfloat16
I32 = mybir.dt.int32
U32 = mybir.dt.uint32
U16 = mybir.dt.uint16
U8 = mybir.dt.uint8
FP8X4 = mybir.dt.float8_e4m3fn_x4
FP4X4 = mybir.dt.float4_e2m1fn_x4
ACT = mybir.ActivationFunctionType
ALU = mybir.AluOpType

P = 128
PACK = 4
HALF = O // 2


def tile_picked_tokens_refinedsome_one_kept_reminder_plain_kernel(
    tc, xt_words, xt_scales, ua, ub, ha, hb, sa, wb_words, wb_scales, xr_words, xr_scales,
    ws_words, ws_scales, offs, offs2, offs3, offs4, offs5, offs6, out,
):
    nc = tc.nc
    with ExitStack() as ctx:
        keep = ctx.enter_context(tc.tile_pool(name="keep", bufs=1))
        psum = ctx.enter_context(tc.psum_pool(name="psum", bufs=1))

        def tiles(name, count, shape, dtype):
            return [keep.tile(shape, dtype, name="%s%d" % (name, c), align_bytes=64) for c in range(count)]

        def load_list(name, src):
            lst = keep.tile(list(src.shape), U16, name=name)
            nc.sync.dma_start(lst[:], src)
            return lst

        def load_column(queue, name, src):
            col = keep.tile([P, PACK], F32, name=name)
            queue.dma_start(col[:], src.rearrange("(p t) o -> p (t o)", t=PACK))
            return col

        def cleared_plane(name, width):
            plane = keep.tile([P, width], U8, name=name, align_bytes=64)
            nc.vector.memset(plane[:].bitcast(I32), 0)
            return plane

        def stage_plane(name, src, width, starts):
            per = 4 // len(starts)
            stage = keep.tile([P, per, width], U8, name=name, align_bytes=64)

            def load(n):
                rows = src[0, 4 * per * n : 4 * per * (n + 1), :].bitcast(I32).rearrange("(q i) c -> i q c", i=4)
                nc.sync.dma_start(stage[starts[n] : starts[n] + 4].bitcast(I32), rows)

            def spread(plane):
                for q in range(4):
                    p0 = starts[q // per]
                    nc.vector.tensor_copy(
                        plane[32 * q : 32 * q + 4, :].bitcast(I32), stage[p0 : p0 + 4, q % per, :].bitcast(I32)
                    )

            return load, spread

        ua_rows = ua.rearrange("(p t) f -> t p f", t=PACK)
        ub_rows = ub.rearrange("(p t) g -> t p g", t=PACK)
        ua_sb = tiles("ua_sb", PACK, [P, F], F32)
        ub_sb = tiles("ub_sb", PACK, [P, G], F32)
        wcd = tiles("wcd", PACK, [P, I], F32)
        wcp = tiles("wcp", PACK, [P, R], F32)
        wca = tiles("wca", PACK, [P, R], F32)

        nc.sync.dma_start(ub_sb[0][:], ub_rows[0])
        hb_sb = load_column(nc.scalar, "hb_sb", hb)
        ha_sb = load_column(nc.scalar, "ha_sb", ha)
        warm = keep.tile([P, 2], F32, name="warm")
        nc.vector.memset(warm[:, 0:1], 0.0)
        nc.scalar.activation(warm[:, 1:2], warm[:, 0:1], ACT.Copy)
        l3 = load_list("l3", offs3)
        l4 = load_list("l4", offs4)
        for t in range(1, PACK - 1):
            nc.sync.dma_start(ub_sb[t][:], ub_rows[t])
        xt_w = keep.tile([P, T], U16, name="xt_w", align_bytes=64)
        nc.sync.dma_start(xt_w[:].bitcast(I32), xt_words[0].bitcast(I32))
        l1 = load_list("l1", offs)
        load_xt, spread_xt = stage_plane("xt_st", xt_scales, T, (0, 64))
        load_xt(0)
        load_xt(1)
        nc.sync.dma_start(ua_sb[0][:], ua_rows[0])
        l2 = load_list("l2", offs2)
        load_wb, spread_wb = stage_plane("wb_st", wb_scales, N, (0,))
        load_wb(0)
        load_ws, spread_ws = stage_plane("ws_st", ws_scales, N, (0,))
        load_ws(0)
        nc.sync.dma_start(ua_sb[1][:], ua_rows[1])
        l6 = load_list("l6", offs6)
        load_xr, spread_xr = stage_plane("xr_st", xr_scales, Z, (0, 64))
        load_xr(0)
        load_xr(1)
        nc.sync.dma_start(ua_sb[2][:], ua_rows[2])
        nc.sync.dma_start(ub_sb[3][:], ub_rows[3])
        nc.sync.dma_start(ua_sb[3][:], ua_rows[3])
        xr_w = keep.tile([P, Z], U32, name="xr_w", align_bytes=64)
        nc.sync.dma_start(xr_w[:].bitcast(I32), xr_words[0].rearrange("p z t -> p (z t)").bitcast(I32))
        l5 = load_list("l5", offs5)
        sa_sb = load_column(nc.sync, "sa_sb", sa)
        ws_w = keep.tile([P, 2 * N], U8, name="ws_w", align_bytes=64)
        nc.sync.dma_start(ws_w[:].bitcast(I32), ws_words[0].bitcast(I32))
        wb_w = keep.tile([P, N], U32, name="wb_w", align_bytes=64)
        nc.sync.dma_start(wb_w[:].bitcast(I32), wb_words[0].rearrange("p n t -> p (n t)").bitcast(I32))

        for t in range(PACK):
            nc.vector.memset(wcp[t][:], 0.0)
        xt_s = cleared_plane("xt_s", T)
        xr_s = cleared_plane("xr_s", Z)
        wb_s = cleared_plane("wb_s", N)
        ws_s = cleared_plane("ws_s", N)

        wc_first = keep.tile([P, PACK - 1, R], BF16, name="wc_first", align_bytes=64)
        wc_bf = tiles("wc_bf", PACK, [P, P, PACK], BF16)
        wc_w = tiles("wc_w", PACK, [P, P], U32)
        wc_s = tiles("wc_s", PACK, [P, P], U8)
        acc = [[psum.tile([P, J // 2], F32, name="acc%d%d" % (c, v)) for v in range(2)] for c in range(PACK)]

        def place_details(t):
            nc.scalar.activation(wcd[t][:], ub_sb[t][:].indirect(l3[:]), ACT.Copy, scale=hb_sb[:, t : t + 1])
            nc.scalar.activation(wcp[t][:].indirect(l4[:]), wcd[t][:], ACT.Copy)

        for t in range(PACK - 1):
            place_details(t)

        def look_up_rows(t):
            nc.scalar.activation(wca[t][:], ua_sb[t][:].indirect(l2[:]), ACT.Copy, scale=ha_sb[:, t : t + 1])
            if t < PACK - 1:
                nc.vector.tensor_tensor(wc_first[:, t, :], wca[t][:], wcp[t][:], ALU.add)

        xg_w = keep.tile([P, J], U16, name="xg_w", align_bytes=64)
        nc.vector.tensor_copy(xg_w[:], xt_w[:].indirect(l1[:]))
        spread_xt(xt_s)
        xg_s = keep.tile([P, J], U8, name="xg_s", align_bytes=64)
        nc.vector.tensor_copy(xg_s[:], xt_s[:].indirect(l1[:]))
        spread_wb(wb_s)
        spread_ws(ws_s)
        spread_xr(xr_s)
        rg_s = keep.tile([P, O], U8, name="rg_s", align_bytes=64)
        nc.vector.tensor_copy(rg_s[:], xr_s[:].indirect(l6[:]))
        for t in range(PACK - 1):
            look_up_rows(t)
        for c in range(PACK):
            nc.vector.tensor_copy(
                wc_bf[c][:, :, 0 : PACK - 1],
                wc_first[:].rearrange("p t (m c) -> p c m t", c=PACK)[:, c, :, :],
            )
        last = PACK - 1
        place_details(last)
        look_up_rows(last)
        codes = wca[last][:].rearrange("p (m c) -> p m c", c=PACK)
        details = wcp[last][:].rearrange("p (m c) -> p m c", c=PACK)
        nc.vector.tensor_tensor(wc_bf[0][:, :, last], codes[:, :, 0], details[:, :, 0], ALU.add)
        wc_last = keep.tile([P, PACK - 1, P], BF16, name="wc_last", align_bytes=64)
        nc.vector.tensor_tensor(
            wc_last[:].rearrange("p c m -> p m c"), codes[:, :, 1:PACK], details[:, :, 1:PACK], ALU.add
        )
        for c in range(PACK):
            if c == 2:
                nc.vector.tensor_copy(wc_bf[c][:, :, last], wc_last[:, c - 1, :])
            elif c > 0:
                nc.scalar.copy(wc_bf[c][:, :, last], wc_last[:, c - 1, :])
            nc.vector.quantize_mx(
                out=wc_w[c][:].bitcast(FP8X4), scales=wc_s[c][:],
                in_=wc_bf[c][:].rearrange("p m t -> p (m t)"),
            )
            for v in range(2):
                slots = slice(v * J // 2, (v + 1) * J // 2)
                nc.tensor.matmul_mx(
                    out=acc[c][v][:], lhsT=wc_w[c][:].bitcast(FP8X4), lhsT_scale=wc_s[c][:],
                    rhs=xg_w[:, slots].bitcast(FP4X4), rhs_scale=xg_s[:, slots], start=True, stop=True,
                )

        g1 = tiles("g1", PACK, [P, J], F32)
        hid = keep.tile([P, PACK, O], BF16, name="hid", align_bytes=64)
        for c in range(PACK):
            for v in range(2):
                slots = slice(v * J // 2, (v + 1) * J // 2)
                if c == 0:
                    nc.scalar.activation(g1[c][:, slots], acc[c][v][:], ACT.Relu)
                else:
                    nc.vector.tensor_scalar_max(g1[c][:, slots], acc[c][v][:], 0.0)
            pieces = [(0, O)] if c < PACK - 1 else [(0, HALF), (HALF, O)]
            for lo, hi in pieces:
                nc.scalar.activation(
                    hid[:, c, lo:hi], g1[c][:].indirect(l5[:, lo // 16 : hi // 16]), ACT.Copy,
                    scale=sa_sb[:, c : c + 1],
                )

        rg_w = keep.tile([P, O], U32, name="rg_w", tag="g10", align_bytes=64)
        nc.vector.tensor_copy(rg_w[:], xr_w[:].indirect(l6[:]))
        res = [[psum.tile([P, HALF], F32, name="res%d%d" % (u, h), tag="acc%d%d" % (u, h)) for h in range(2)] for u in range(2)]
        for u in range(2):
            cols = slice(u * HALF, (u + 1) * HALF)
            for h in range(2):
                nc.tensor.matmul_mx(
                    out=res[u][h][:], lhsT=ws_w[:, 2 * P * h : 2 * P * (h + 1)].bitcast(FP4X4),
                    lhsT_scale=ws_s[:, P * h : P * (h + 1)],
                    rhs=rg_w[:, cols].bitcast(FP8X4), rhs_scale=rg_s[:, cols], start=True, stop=False,
                )

        hid_bf = tiles("hid_bf", 2, [P, HALF, PACK], BF16)
        hid_w = tiles("hid_w", 2, [P, HALF], U32)
        hid_s = tiles("hid_s", 2, [P, HALF], U8)
        out_sb = [tiles("out_sb%d" % u, 2, [P, HALF], F32) for u in range(2)]
        for u in range(2):
            cols = slice(u * HALF, (u + 1) * HALF)
            nc.vector.tensor_copy(hid_bf[u][:], hid[:, :, cols].rearrange("p c o -> p o c"))
            nc.vector.quantize_mx(
                out=hid_w[u][:].bitcast(FP8X4), scales=hid_s[u][:],
                in_=hid_bf[u][:].rearrange("p o c -> p (o c)"),
            )
            for h in range(2):
                nc.tensor.matmul_mx(
                    out=res[u][h][:], lhsT=wb_w[:, P * h : P * (h + 1)].bitcast(FP8X4),
                    lhsT_scale=wb_s[:, P * h : P * (h + 1)],
                    rhs=hid_w[u][:].bitcast(FP8X4), rhs_scale=hid_s[u][:], start=False, stop=True,
                )
                if u == 1 and h == 1:
                    nc.vector.tensor_copy(out_sb[u][h][:], res[u][h][:])
                else:
                    nc.scalar.copy(out_sb[u][h][:], res[u][h][:])
                queue = nc.scalar if (u == 1 and h == 0) else nc.sync
                queue.dma_start(out[P * h : P * (h + 1), cols], out_sb[u][h][:])
